import numpy as np, ml_dtypes
CORES = [16,32,48,64,80]
N = 5
BF = ml_dtypes.bfloat16
def gentries(a):
    return np.ascontiguousarray(a.reshape(8, 16, -1).transpose(0, 2, 1)).reshape(8, -1)
def gtable(e):
    e = np.asarray(e); return np.ascontiguousarray(e.reshape(8, -1, 16).transpose(0, 2, 1)).reshape(128, -1).astype(np.int32)
V, B, L = 2560, 64, 2
W = V + (N - 1) * B
def parts(rng):
    x = (3 * rng.integers(0, 256, (N, 8, 1, V)) + rng.integers(0, 256, (N, 8, 16, V)) + rng.integers(0, 2, (N, 8, 16, V))) >> 2
    t = rng.integers(1, 97, (N, 8, 16, 1)); nx = np.argsort(rng.random((N, 8, 2 * W)), axis=-1)
    sh = np.argsort(rng.random((N, 8, N - 1, V)), axis=-1)[..., :B]
    return np.minimum(x, 255), t, np.ascontiguousarray(nx), np.ascontiguousarray(sh)
def both(rng, a):
    w = rng.integers(0, 2, (len(a), 1)); return 2 * a[:, None] + np.concatenate([w, 1 - w], axis=1)
def chains(rng, g, x, t, nx, sh):
    K = min(B, (V - B) // (3 * N) // 32 * 32); n = N * K
    t[:, g] = 256 * (N - 1) + 1; o = np.argsort(rng.random((N, N - 1, B)), axis=2)
    s = np.stack([3 * n + rng.permutation(V - 3 * n)[:B] for q in range(N)])
    for q in range(N):
        sh[q, g] = s[q][o[q]]
    for r in range(N):
        u = np.concatenate([s[r, :K]] + [V + (d - 1) * B + np.flatnonzero(o[(r - d) % N, d - 1] < K) for d in range(1, N)])
        m = rng.permutation(2 * n); a = m[:n]; e = m[n:]; b = 2 * n + rng.permutation(n)
        x[r, g][:, m] = 0; x[r, g][:, b] = 255; x[r, g][:, s[r, :K]] = 255
        nx[r, g] = np.arange(2 * W)
        for i, j in ((u, a), (a, b), (b, e), (e, u)):
            w = rng.integers(0, 2, n); nx[r, g, 2 * i] = 2 * j + w; nx[r, g, 2 * i + 1] = 2 * j + 1 - w
def put(rng, y, p, nodes, order, high):
    v = rng.integers(0, 4, (4, len(nodes))); y[:, nodes] = order; y[np.ix_(p, nodes)] = 255 - v if high else v
def swell(rng, g, x, t, nx, sh):
    K = 32; n = N * K; m = N * 8; lo = 4 * n
    p = rng.permutation(16)[:4]; t[:, g, p[:2]] = 4095; t[:, g, p[2]] = 0; t[:, g, p[3]] = 301
    o = np.argsort(rng.random((N, N - 1, B)), axis=2); s = np.stack([lo + rng.permutation(V - lo)[:B] for q in range(N)]); one = int(rng.integers(0, N))
    for q in range(N):
        sh[q, g] = s[q][o[q]]
    for r in range(N):
        u = rng.permutation(np.concatenate([s[r, :K]] + [V + (d - 1) * B + np.flatnonzero(o[(r - d) % N, d - 1] < K) for d in range(1, N)]))
        w = rng.permutation(lo); v = x[r, g]; y = nx[r, g]; y[:] = np.arange(2 * W); put(rng, v, p, s[r, :K], 0, True)
        if r != one:
            a = w[:n]; e = w[n:2 * n]; b = w[2 * n:3 * n]
            put(rng, v, p, w[:2 * n], 127, False); put(rng, v, p, b, 254, True)
            for i, j in ((u, a), (a, b), (b, e), (e, u)):
                y[both(rng, i)] = both(rng, j)
        else:
            c = w[:m]; zh = w[m:2 * m]; zl = w[2 * m:3 * m]; f1 = w[3 * m:5 * m]; f2 = w[5 * m:7 * m]; a1 = w[7 * m:10 * m]; a2 = w[10 * m:13 * m]; b = w[13 * m:16 * m]
            for i, k, h in ((c, 254, True), (zh, 254, False), (zl, 0, False), (f1, 127, True), (f2, 127, True), (a1, 127, False), (a2, 127, False), (b, 254, True)):
                put(rng, v, p, i, k, h)
            ui = both(rng, u); uo = both(rng, u)
            i = both(rng, f1); j = both(rng, f1)
            y[both(rng, c).ravel()] = i[:, 0]; y[both(rng, zh).ravel()] = i[:, 1]; y[j[:, 0]] = ui[:2 * m, 0]; y[j[:, 1]] = both(rng, zl).ravel()
            i = both(rng, f2); j = both(rng, f2)
            y[uo[2 * m:, 0]] = i[:, 0]; y[both(rng, zl).ravel()] = i[:, 1]; y[j[:, 0]] = both(rng, c).ravel(); y[j[:, 1]] = both(rng, zh).ravel()
            i = np.concatenate([ui[:2 * m, 1], ui[2 * m:].ravel()]); j = np.concatenate([uo[:2 * m].ravel(), uo[2 * m:, 1]])
            y[both(rng, b).ravel()] = rng.permutation(both(rng, a1).ravel()); y[both(rng, a1).ravel()] = rng.permutation(i)
            y[j] = rng.permutation(both(rng, a2).ravel()); y[both(rng, a2).ravel()] = rng.permutation(both(rng, b).ravel())
def crowd(rng, g, x, nx, sh, two):
    k = W // 5 if two else W // 2; lo = 3 * k if two else k
    x[:, g] = rng.integers(0, 256, (16, 1))
    for q in range(N):
        s = lo + rng.permutation(V - lo)[:B]; y = nx[q, g]; y[:] = np.arange(2 * W)
        for d in range(N - 1): sh[q, g, d] = rng.permutation(s)
        if two:
            ab = k + rng.permutation(2 * k); ce = 3 * k + rng.permutation(2 * k); five = (rng.permutation(k), ab[:k], ab[k:], ce[:k], ce[k:])
            om, oa, ob, oc, oe = [both(rng, z) for z in five]; im, ia, ib, ic, ie = [both(rng, z) for z in five]
            y[oa[:, 0]] = im[:, 0]; y[oa[:, 1]] = ic[:, 1]; y[ob[:, 0]] = im[:, 1]; y[ob[:, 1]] = ie[:, 1]; y[om[:, 0]] = ic[:, 0]; y[om[:, 1]] = ie[:, 0]
            y[oc[:, 0]] = ia[:, 0]; y[oc[:, 1]] = ib[:, 0]; y[oe[:, 0]] = ia[:, 1]; y[oe[:, 1]] = ib[:, 1]
        else:
            a = rng.permutation(k); b = k + rng.permutation(k)
            y[both(rng, a)] = both(rng, b); y[both(rng, b)] = both(rng, a)
def pack(x, t, nx, sh):
    return {"x0": np.ascontiguousarray(x.reshape(N, 128, V)).astype(np.int32), "th": np.ascontiguousarray(t.reshape(N, 128, 1)).astype(np.int32),
            "nxt": np.stack([gtable(a) for a in nx]), "shw": np.stack([gtable(a.reshape(8, -1)) for a in sh])}
def setup_inputs(rng):
    return pack(*parts(rng))
def setup_inputs_flat(rng):
    x, t, nx, sh = parts(rng)
    x[:, 0] = 255; x[:, 2] = rng.integers(0, 2, (N, 16, V)); x[:, 3] = 255 * rng.integers(0, 2, (N, 16, V))
    x[:, 4] = 255 * rng.integers(0, 2, (N, 1, V)); x[:, 5] = rng.integers(0, 4, (N, 1, V)); x[:, 6] = 64 * rng.integers(0, 4, (N, 16, V))
    v = np.array([0, 1, 2, 63, 64, 65, 127, 128, 129, 191, 192, 255, 256])
    t[:, ::2] = rng.choice(v, (N, 4, 16, 1)); t[:, 3] = rng.choice(v, (N, 16, 1)); t[:, 5] = rng.choice(np.array([0, 1, 2, 3]), (N, 16, 1))
    crowd(rng, 1, x, nx, sh, True); crowd(rng, 7, x, nx, sh, False)
    return pack(x, t, nx, sh)
def setup_inputs_loops(rng):
    x, t, nx, sh = parts(rng); p = np.arange(2 * W)
    for q in range(N):
        nx[q, 1] = p; nx[q, 2] = (p ^ 2) ^ np.repeat(rng.integers(0, 2, W), 2)
        nx[q, 3] = (p + 2) % (2 * W); nx[q, 5] = np.where(p & 1 == 0, (p + 2) % (2 * W), (p - 2) % (2 * W))
        i = np.flatnonzero(rng.random(2 * W) < 0.5); nx[q, 6] = p; nx[q, 6, i] = rng.permutation(i)
    chains(rng, 0, x, t, nx, sh); chains(rng, 4, x, t, nx, sh); swell(rng, 7, x, t, nx, sh)
    return pack(x, t, nx, sh)
def setup_inputs_ends(rng):
    x, t, nx, sh = parts(rng); k = 2 * (N - 1) * B
    for q in range(N):
        for g in range(8):
            if g % 2 == 0:
                s = np.concatenate([np.array([0, V - 1]), 1 + rng.permutation(V - 2)[:B - 2]])
                for d in range(N - 1): sh[q, g, d] = rng.permutation(s)
            else:
                sh[q, g] = V - 1 - np.arange((N - 1) * B).reshape(N - 1, B)
            if g in (0, 3, 4):
                o = rng.permutation(2 * V); nx[q, g, 2 * V:] = o[:k]
                nx[q, g, :2 * V] = rng.permutation(np.concatenate([o[k:], np.arange(2 * V, 2 * W)]))
            if g == 5:
                nx[q, g] = np.concatenate([rng.permutation(2 * V), 2 * V + rng.permutation(k)])
    return pack(x, t, nx, sh)
def setup_inputs_uneven(rng):
    x, t, nx, sh = parts(rng); q = rng.permutation(N)
    x[q[0]] = rng.integers(0, 4, (8, 16, V)); t[q[1]] = 4095; t[q[2]] = 0; x[q[3]] = 255 * rng.integers(0, 2, (8, 16, V))
    return pack(x, t, nx, sh)
def setup_inputs_spread(rng):
    x, t, nx, sh = parts(rng)
    x = np.minimum((np.exp2(8 * rng.random((N, 8, 1, V))) * rng.random((N, 8, 16, V))).astype(np.int64), 255)
    t = np.minimum(np.exp2(12 * rng.random((N, 8, 16, 1))).astype(np.int64) - 1, 4095)
    return pack(x, t, nx, sh)
def check_inputs(d):
    bad = []
    for k, lo, hi in (("x0", 0, 255), ("th", 0, 4095), ("nxt", 0, 2 * W - 1), ("shw", 0, V - 1)):
        if np.min(d[k]) < lo or np.max(d[k]) > hi: bad.append("range of " + k)
    if any(np.any(np.sort(gentries(a), axis=1) != np.arange(2 * W)) for a in d["nxt"]): bad.append("nxt holds each number once")
    s = np.sort(np.stack([gentries(a) for a in d["shw"]]).reshape(N, 8, N - 1, B), axis=3)
    if np.any(s[..., 1:] == s[..., :-1]): bad.append("different nodes in a block of shw")
    return bad
def reference(x0, th, nxt, shw):
    x = np.zeros((N, 8, 16, W), np.int32); x[..., :V] = x0.reshape(N, 8, 16, V); t = th.astype(np.int32).reshape(N, 8, 16, 1)
    nx = np.stack([gentries(a) for a in nxt]).astype(np.int64); pv = np.argsort(nx, axis=2)
    sh = np.stack([gentries(a) for a in shw]).astype(np.int64).reshape(N, 8, N - 1, B)
    border = np.zeros((N, 8, V), bool); np.put_along_axis(border, sh.reshape(N, 8, -1), True, 2)
    may = np.zeros((N, 8, W), bool); may[..., :V] = ~border
    inn = np.ones((N, 8, W), bool); port = np.arange(2 * W)
    def pick(a, ports):
        return np.take_along_axis(a, (ports >> 1)[:, :, None, :], 3)
    def sum4(a, n, p):
        b = pick(a, p) + pick(a, n); return b[..., 0::2] + b[..., 1::2]
    def size(u):
        return np.add.reduce(np.minimum(np.abs(u), 255), axis=2)
    def outward(a):
        for r in range(N):
            for d in range(1, N):
                q = (r - d) % N
                a[r, :, :, V + (d - 1) * B:V + d * B] = np.take_along_axis(a[q], sh[q, :, d - 1][:, None, :], 2)
    def home(s):
        o = s[..., :V].copy()
        for r in range(N):
            for d in range(1, N):
                q = (r - d) % N; ix = sh[q, :, d - 1][:, None, :]
                np.put_along_axis(o[q], ix, np.take_along_axis(o[q], ix, 2) + s[r, :, :, V + (d - 1) * B:V + d * B], 2)
        return o
    det = np.zeros((N, 8, 16, W), np.int32); kept = []
    for lev in range(L):
        outward(x)
        a = pick(x, pv); b = pick(x, nx); a0, a1, b0, b1 = a[..., 0::2], a[..., 1::2], b[..., 0::2], b[..., 1::2]
        d = x - ((a0 + a1 + b0 + b1) >> 2)
        key = size(d).astype(np.int64) * 4096 + np.arange(W)
        k = np.minimum(np.take_along_axis(key, pv >> 1, 2), np.take_along_axis(key, nx >> 1, 2))
        lv = may & (key < np.minimum(k[..., 0::2], k[..., 1::2]))
        c = size(a0 - b1) + size(a1 - b0) < size(a0 - b0) + size(a1 - b1)
        s = np.where(lv[:, :, None, :], d >> 2, 0).astype(np.int32)
        x[..., :V] += home(sum4(s, nx, pv)) * inn[:, :, None, :V]
        det = np.where(lv[:, :, None, :], d, det); kept.append((lv, nx, pv, inn))
        l2 = np.repeat(lv, 2, axis=2); other = port ^ np.repeat(c, 2, axis=2).astype(np.int64)
        fn = np.where(l2, np.take_along_axis(nx, other, 2), port); fp = np.where(l2, np.take_along_axis(pv, other, 2), port)
        nx = np.take_along_axis(fn, nx, 2); pv = np.take_along_axis(fp, pv, 2)
        may = may & ~lv; inn = inn & ~lv
    det = np.where(np.abs(det) < t, 0, det).astype(np.int32)
    for lv, n, p, was in kept[::-1]:
        s = np.where(lv[:, :, None, :], det >> 2, 0).astype(np.int32)
        x[..., :V] -= home(sum4(s, n, p)) * was[:, :, None, :V]
        outward(x)
        x = np.where(lv[:, :, None, :], det + (sum4(x, n, p) >> 2), x).astype(np.int32)
    return {"yx": np.ascontiguousarray(x[..., :V]).reshape(N, 128, V).astype(np.float32), "yn": nx.astype(np.float32)}

from concourse.bass import DstId, RemoteDMATransfer
from concourse.mybir import dt, AluOpType, ActivationFunctionType

OP = AluOpType
AF = ActivationFunctionType
N, V, W, B = 5, 2560, 2816, 64
CW, CV = 176, 160
WZ = W + 16
K = 4096.0
M1, M4, M16, M256 = 1.5 * 2 ** 23, 1.5 * 2 ** 21, 1.5 * 2 ** 19, 1.5 * 2 ** 31
BIG = 2.0 ** 26
MID = 8192.0 * 2040
MAIN = {"g": 1.56, "sc": 3.8, "pe": 0.5, "rem": 5000.0, "hop": 120.0}
OTHER = ({"g": 1.15, "sc": 2.2, "pe": 0.6, "rem": 4000.0, "hop": 200.0}, {"g": 2.0, "sc": 5.5, "pe": 0.45, "rem": 8000.0, "hop": 80.0})
COST = dict(MAIN)
KNOBS = {"nS": (2816,), "s3": (1, 2, 0), "su": (2, 1), "sf": (2, 1), "px": (4, 2), "ph": (9, 6), "sig": (1, 0), "rD0": (0,),
         "rU": (0, 2, 6), "rDQ": (2, 0), "rH": (1, 0), "rO": (0, 1), "cV": (0,), "lat0": (0, 1), "lat1": (1, 0), "vpen": (500.0, 200.0)}
ROUNDS = 3000


def _layout(items):
    at, o = {}, 0
    for n, w in items:
        at[n] = o
        o += (w + 15) // 16 * 16
    return at, o


_BF, _nBF = _layout([("XB", W), ("GB", 4 * W), ("GR", 5120), ("RL", 2 * W), ("D0", WZ), ("AB", W), ("DS", WZ), ("F0", V),
                     ("H0", V), ("TMP", 1024), ("HI", 704), ("LO", 704), ("S0", 256), ("ZZ", 576), ("I1", 128), ("In1", 128),
                     ("Inh", 128), ("Inq", 128), ("I256", 128), ("I16", 128), ("Ink", 128), ("CR", 384), ("ONE", 512)])
_F, _nF = _layout([("SA", 2 * WZ), ("SB", 2 * W), ("X1", W), ("Y1", W), ("IO", W), ("Gf", 352), ("Q", 704), ("QK", 704), ("E", 704),
                   ("T1", 352), ("T2", 352), ("NN", 352), ("P2", 352), ("NM", 160), ("NZ", 160), ("C", 176), ("MN", 160), ("KO", 160),
                   ("If", 128), ("I4", 128), ("Ifn", 128), ("LV", 352), ("COL", 16), ("T8", 16), ("BT", 64), ("BU", 64), ("HS0", 256),
                   ("HP0", 256), ("HS1", 256), ("E1", 256), ("E2", 256), ("E3", 256), ("LS0", 256), ("LP0", 256), ("LS1", 256)])
_I, _nI = _layout([("X0", V), ("G", 352), ("J1", 352), ("J2", 352), ("SH", 16), ("J3", 16), ("J4", 16), ("TH", 16), ("PC", 16)])
_U, _nU = _layout([("POSN", 352), ("POSP", 352), ("POS1", 352), ("U0", 704), ("U1", 704), ("US0", 704), ("US1", 704),
                   ("LM", 160), ("SHU", 16), ("SHP", 16)])
_H, _nH = _layout([("GH", 4 * W), ("J1h", 128), ("Jn1", 128), ("Jn16", 128)])
SCRATCH = {"bf": ("sbuf", [128, _nBF], "bfloat16"), "fl": ("sbuf", [128, _nF], "float32"), "it": ("sbuf", [128, _nI], "int32"),
           "us": ("sbuf", [128, _nU], "uint16"), "hf": ("sbuf", [128, _nH], "float16")}
for _b in range(8):
    SCRATCH["ps%d" % _b] = ("psum", [128, 512], "float32")
WHERE = {}
for _buf, _at in (("bf", _BF), ("fl", _F), ("it", _I), ("us", _U), ("hf", _H)):
    for _n in _at:
        WHERE[_n] = (_buf, _at[_n])
for _n, _o, _d in (("DQ", "SA", 0), ("A32", "SA", WZ), ("FN1", "SA", 0), ("DC", "SB", 0), ("H1", "SB", W), ("YN", "SB", 0),
                   ("BW", "Y1", 0), ("OUT", "Y1", 0), ("Y0", "X1", 0), ("WN", "AB", 0), ("SP", "DS", 0), ("PSI", "D0", 0),
                   ("PM", "X1", 0), ("O", "X1", 512), ("ZT", "X1", 640), ("IO2", "X1", 1024), ("CUT", "F0", 0), ("FN", "RL", 0),
                   ("TA", "E", 0), ("TB", "E", 352)):
    WHERE[_n] = (WHERE[_o][0], WHERE[_o][1] + _d)
SEMAPHORES = ["cV", "cS", "cP", "cG", "ls", "r0", "r1", "r2", "r3", "r4", "r5", "r6"] + ["d%d" % i for i in range(40)]
TWO = ("bf", "hf", "us")
PLAN = {}


def r(n, a, b, s=1):
    if n[:2] == "ps":
        return (n, a, b, s)
    return (WHERE[n][0], WHERE[n][1] + a, WHERE[n][1] + b, s)


def cnt(x):
    return (x[2] - x[1] + x[3] - 1) // x[3]


def build(g, T, topo, rank, cfg):
    ops = []

    def ap(x):
        return T[x[0]][:, x[1]:x[2]:x[3]] if x[3] != 1 else T[x[0]][:, x[1]:x[2]]

    def rows(x, role):
        return T[x[0]][role:128:16, x[1]:x[2]]

    def add(eng, cost, fn, rd, wr, lat=0.0, kind="c", tag=None, after=None, sem=None):
        ops.append({"eng": eng, "cost": cost, "fn": fn, "rd": [x for x in rd if isinstance(x, tuple)], "wr": wr, "lat": lat,
                    "kind": kind, "tag": tag, "after": after, "sem": sem})
        return len(ops) - 1

    def sc(x):
        return ap(x) if isinstance(x, tuple) else x

    def src(i, off):
        return ap(i) if off is None else ap(i).indirect(ap(off))

    def ucost(o, i, off=None):
        n = cnt(o)
        if off is not None:
            return {"V": 60 + n * COST["g"], "S": 75 + n * COST["g"]}
        return {"V": 60 + max(64, n * (0.5 if (o[0] in TWO and i[0] in TWO) else 1.0)), "S": 75 + max(64, n)}

    def lin(o, i, mul=1.0, plus=0.0, off=None, eng="VS"):
        def fn(e):
            if e == "S":
                return g.scalar.activation(ap(o), src(i, off), AF.Identity, bias=plus, scale=mul)
            if mul == 1.0 and plus == 0.0:
                return g.vector.tensor_copy(ap(o), src(i, off))
            return g.vector.tensor_scalar(ap(o), src(i, off), mul, plus, OP.mult, OP.add)
        add(eng, ucost(o, i, off), fn, [i, off], [o])

    def act(o, i, func, mul=1.0, plus=0.0):
        add("S", ucost(o, i), lambda e: g.scalar.activation(ap(o), ap(i), func, bias=sc(plus), scale=mul), [i, plus], [o])

    def relu(o, i, eng="VS"):
        def fn(e):
            if e == "S":
                return g.scalar.activation(ap(o), ap(i), AF.Relu)
            return g.vector.tensor_scalar(ap(o), ap(i), 0.0, None, OP.max)
        add(eng, ucost(o, i), fn, [i], [o])

    def ts(o, i, s1, o1, s2=None, o2=None):
        def fn(e):
            if s2 is None:
                return g.vector.tensor_scalar(ap(o), ap(i), sc(s1), None, o1)
            return g.vector.tensor_scalar(ap(o), ap(i), sc(s1), sc(s2), o1, o2)
        add("V", ucost(o, i), fn, [i, s1, s2], [o])

    def tt(o, a, b, op, off=None):
        f = COST["g"] if off is not None else (1.0 if "ps" in (a[0][:2], b[0][:2]) else 2.0)
        add("V", {"V": 60 + max(64, cnt(o) * f)}, lambda e: g.vector.tensor_tensor(ap(o), src(a, off), ap(b), op), [a, b, off], [o])

    def rnd(o, i, m, on_s, t=None):
        if on_s:
            lin(t or i, i, 1.0, m, eng="S")
            lin(o, t or i, 1.0, -m, eng="S")
        else:
            ts(o, i, m, OP.add, m, OP.subtract)

    def ms(o, c):
        add("V", ucost(o, o), lambda e: g.vector.memset(ap(o), c), [], [o])

    def scat(win, off, i, plus=None, eng="V"):
        def fn(e):
            o = ap(win).indirect(ap(off))
            if e == "S":
                return g.scalar.activation(o, ap(i), AF.Silu)
            if plus is None:
                return g.vector.tensor_copy(o, ap(i))
            return g.vector.tensor_scalar(o, ap(i), 1.0, plus, OP.mult, OP.add)
        add(eng, {eng: 70 + cnt(i) * COST["sc"]}, fn, [i, off], [win])

    def mm(o, terms, start=True, stop=True):
        def fn(e):
            last = None
            for j, t in enumerate(terms):
                l, x = ap(t[0]), ap(t[1])
                if len(t) == 3:
                    l, x = T[t[0][0]][0:1, t[0][1]:t[0][2]], T[t[1][0]][0:1, t[1][1]:t[1][2]]
                last = g.tensor.matmul(ap(o), l, x, start and j == 0, stop and j == len(terms) - 1)
            return last
        c = sum(20 + max(64, cnt(o)) * COST["pe"] * (4 if t[1][0] == "fl" else 1) for t in terms)
        add("P", {"P": c}, fn, [t[0] for t in terms] + [t[1] for t in terms], [o])

    def wrap(o, parts, first=None):
        terms = [(r("If", 0, 128), first)] if first else []
        for z, n, a, step in parts:
            for i in range(16):
                s = a + i * (step // 16)
                terms.append((r("ZZ", 144 * z + 15 - i, 144 * z + 143 - i), r(n, s, s + (cnt(o) - 1) * step + 1, step)))
        mm(o, terms)

    def pool(o, fn, rd):
        add("G", {"G": 170 + 2 * cnt(o)}, fn, rd, [o])

    def pick(o, i, pat, op, base, cm):
        pool(o, lambda e: g.affine_select(ap(o), ap(i), pat, op, 0.0, base, cm), [i])

    def cast(o, i):
        pick(o, i, [[0, cnt(o)]], OP.is_ge, 0, 0)

    nd = [0]

    def dma(q, o, i, rd, wr, nbytes, tag=None):
        nd[0] += 1
        add(q, {q: 100.0}, lambda e: (g.sync if e == "Y" else g.scalar).dma_start(o, i), rd, wr, lat=2000 + nbytes / 200.0,
            kind="dma", tag=tag, sem="d%d" % nd[0])

    def fold(tab, win, role=0):
        dma("Y", ap(tab), rows(win, role), [win], [tab], 128 * cnt(tab) * 4)

    def unfold(win, tab, role=0):
        dma("Y", rows(win, role), ap(tab), [tab], [win], 128 * cnt(tab) * 4, tag=role)

    def send(sb, land, a, sem, home):
        def fn(e):
            tr = []
            for d in range(1, N):
                dst = T.cores[(rank - d) % N if home else (rank + d) % N]
                en = topo.engines(T.cores[rank], dst)
                per = len(en) // (N - 1)
                rid, pid, _ = topo.addr(dst)
                tr.append(RemoteDMATransfer(dst_ids=[DstId(rid=rid, pnc=pid)], dma_engine_mask=sum(1 << x for x in en[(d - 1) * per:d * per]),
                                            remote_sem=T.sem[sem], src=ap(r(sb, (d - 1) * B, d * B)),
                                            dst=ap(r(land, a + (d - 1) * B, a + d * B))))
            return g.remote_dma_fused(tr, local_sem=T.sem.ls)
        k = add("G", {"G": 500.0}, fn, [r(sb, 0, 256)], [], kind="send")
        add("", {}, None, [], [r(land, a, a + 256)], lat=COST["rem"] + (3000 if sem == "r0" else 0), kind="recv", after=k, sem=sem)

    bank = [0, 0]

    def nb(n, aux=0):
        bank[aux] += 1
        return r("ps%d" % ((3, 7)[bank[1] % 2] if aux else bank[0] % 3), 0, n)

    ring = [0]

    def slot(n):
        ring[0] += 1
        return r("IO", 512 * (ring[0] % 5), 512 * (ring[0] % 5) + n)

    def lst(u, k, a, b):
        return r(u, CW * k + a // 16, CW * k + b // 16)

    OWN = [(a, a + 512) for a in range(0, V, 512)]
    GHO = [(V, W)]
    HALF = ((0, 1280), (1280, V))
    THIRD = ((0, 512), (512, 1024), (1024, 1280))
    col = lambda j: r("COL", j, j + 1)
    I = lambda n: r(n, 0, 128)
    t2 = lambda n, j: r(n, 352 * j, 352 * j + 352)
    nS = cfg["nS"]
    io = lambda a, b: r("IO", a, b) if b <= W else r("IO2", a - W, b - W)
    SA, SB, FN = r("SA", 0, 2 * W), r("SB", 0, 2 * W), r("FN", 0, 2 * W)

    dma("Y", ap(t2("G", 0)), T.nxt[:], [], [t2("G", 0)], 180224)
    dma("S", ap(r("SH", 0, 16)), T.shw[:], [], [r("SH", 0, 16)], 8192)
    ms(t2("ZT", 0), 0.0)
    unfold(SB, t2("ZT", 0), 0)
    unfold(SA, t2("ZT", 0), 0)
    dma("S", ap(r("X0", 0, V)), T.x0[:], [], [r("X0", 0, V)], 128 * V * 4)
    unfold(r("BW", 0, V), r("ZT", 0, CV), 0)
    dma("Y", ap(r("TH", 0, 1)), T.th[:], [], [r("TH", 0, 1)], 512)
    for a in range(0, nS, 704):
        pool(io(a, a + 704), lambda e, a=a: g.iota(ap(io(a, a + 704)), [[1, 704]], a + 32, 0, allow_small_or_imprecise_dtypes=True), [])

    def pos(o, i, n, sh, mul, j1, j2):
        ts(r(j1, 0, n), i, sh, OP.arith_shift_right)
        ts(r(j2, 0, n), i, (1 << sh) - 1, OP.bitwise_and)
        ts(r(j2, 0, n), r(j2, 0, n), mul, OP.mult)
        tt(r(j1, 0, n), r(j1, 0, n), r(j2, 0, n), OP.add)
        lin(o, r(j1, 0, n), eng="V")
    pos(t2("POSN", 0), t2("G", 0), 352, 5, CW, "J1", "J2")
    for a in range(0, 2 * W, 704):
        o = r("POSN", a // 16, a // 16 + 44)
        if a < nS:
            scat(SB, o, io(a, a + 704), eng="S")
        else:
            scat(SA, o, io(0, 704), plus=float(a))
    lin(r("SHU", 0, 16), r("SH", 0, 16), eng="V")
    lin(r("S0", 0, 256), r("X0", 0, V), off=r("SHU", 0, 16), eng="V")
    send("S0", "XB", V, "r0", False)
    for a in range(0, V, 640):
        if a // 640 < cfg["px"]:
            cast(r("XB", a, a + 640), r("X0", a, a + 640))
        else:
            lin(r("XB", a, a + 640), r("X0", a, a + 640), eng="V")
    ms(I("O"), 1.0)
    for b in range(2):
        for h in range(2):
            pick(r("PM", (2 * b + h) * 128, (2 * b + h + 1) * 128), I("O"), [[-16, 8], [1000 - 2000 * h, 2], [-2, 8]], OP.is_equal, 1000 * h - b, 1)
    pick(I("If"), I("O"), [[-1, 128]], OP.is_equal, 0, 1)
    for n, c in (("I1", 1.0), ("In1", -1.0), ("Inh", -0.5), ("Inq", -0.25), ("I256", 256.0), ("I16", 1 / 16), ("Ink", -1 / 1024),
                 ("I4", 4.0), ("Ifn", -1.0)):
        lin(I(n), I("If"), c)
    for n, c in (("J1h", 1.0), ("Jn1", -1.0), ("Jn16", -1 / 16)):
        lin(I(n), I("If"), c, eng="V")
    for j, c in enumerate((0.375, 3 / 16, -3 / 32)):
        ms(r("CR", 128 * j, 128 * j + 128), c)
    ms(r("ONE", 0, 512), 1.0)
    const = lambda j, n: (r("CR", 128 * j, 128 * j + 128), r("ONE", 0, n), 1)
    ms(r("ZZ", 0, 576), 0.0)
    pick(r("T8", 0, 8), r("O", 0, 8), [[-16, 8]], OP.is_ge, 0, 1)
    pick(r("T8", 8, 16), r("T8", 0, 8), [[16, 8]], OP.is_ge, 15, -1)
    pool(r("PC", 0, 1), lambda e: g.iota(ap(r("PC", 0, 1)), [[1, 1]], 0, 2), [])
    pool(t2("NN", 0), lambda e: g.iota(ap(t2("NN", 0)), [[0, 2], [32, CW]], 0, 0, allow_small_or_imprecise_dtypes=True), [])
    ts(r("PC", 1, 2), r("PC", 0, 1), 31, OP.bitwise_and)
    lin(col(0), r("PC", 1, 2), eng="V")
    ts(col(1), col(0), 4.0, OP.is_lt)
    ts(col(2), col(0), 8.0, OP.is_lt)
    tt(col(2), col(2), col(1), OP.subtract)
    lin(col(3), r("TH", 0, 1), eng="V")
    lin(col(4), col(3), 256.0, -128.0)
    for z, c in enumerate((8192.0, -8192.0, col(1), col(2))):
        ts(r("ZZ", 144 * z + 15, 144 * z + 128, 16), r("T8", 8, 16), c, OP.mult)
    ts(t2("NN", 0), t2("NN", 0), col(0), OP.add)
    for b in range(2):
        lin(r("P2", CW * b, CW * b + CW), r("NN", 0, CW), 1.0, float(b))
    lin(r("NZ", 0, CV), r("NN", 0, CV), 0.5, -float(W))
    ms(t2("LV", 0), 0.0)
    ms(r("C", CV, CW), 0.0)
    ms(r("D0", W, WZ), 0.0)
    ms(r("DS", V, WZ), 0.0)
    lin(t2("Gf", 0), t2("G", 0), eng="V")
    for b in range(2):
        mm(r("ps4", CW * b, CW * b + CW), [(r("PM", (2 * b + h) * 128, (2 * b + h + 1) * 128), r("Gf", h, 352, 2)) for h in range(2)])
    lin(t2("U0", 0), t2("ps4", 0), 0.5, -0.25, eng="V")
    lin(t2("Q", 0), t2("ps4", 0))
    fold(t2("TA", 0), SA)
    fold(t2("TB", 0), SB)
    tt(t2("TA", 0), t2("TA", 0), t2("TB", 0), OP.add)
    lin(t2("U0", 1), t2("TA", 0), 0.5, -16.25, eng="V")
    lin(t2("G", 0), t2("TA", 0), 1.0, -32.0, eng="V")
    lin(t2("Q", 1), t2("G", 0), eng="V")
    pos(t2("POSP", 0), t2("G", 0), 352, 5, CW, "J1", "J2")
    lin(r("QK", 0, 704), r("Q", 0, 704), 1.0, -MID)
    pos(r("SHP", 0, 16), r("SH", 0, 16), 16, 4, CV, "J3", "J4")
    ms(r("BU", 0, 64), BIG)
    for d in range(4):
        scat(r("BW", 0, V), r("SHP", 4 * d, 4 * d + 4), r("BU", 0, 64))
    NM, KO, MN = r("NM", 0, CV), r("KO", 0, CV), r("MN", 0, CV)
    fold(NM, r("BW", 0, V))
    tt(NM, NM, r("P2", CW, CW + CV), OP.add)
    lin(NM, NM, 1.0, -MID)

    def leave(win, u, z):
        for h in range(2):
            wrap(r("ps6", 80 * h, 80 * h + 80), [(z, win, 1280 * h, 16)], r("NM", 80 * h, 80 * h + 80))
        lin(KO, r("ps6", 0, CV))
        for k in range(4):
            p = "ps%d" % (4 + k % 2)
            for h in range(2):
                s = 1280 * ((2 * k + h) % 4)
                lin(r("GR", s, s + 1280), r(win, 0, W), off=lst(u, k, 1280 * h, 1280 * h + 1280))
                wrap(r(p, 80 * h, 80 * h + 80), [(z, "GR", s, 16)], r("QK", CW * k + 80 * h, CW * k + 80 * h + 80))
            if k:
                tt(MN, r(p, 0, CV), MN, OP.min)
            else:
                lin(MN, r(p, 0, CV))
        tt(r("LV", 0, CV), KO, MN, OP.is_lt)
        tt(r("T2", 0, CV), r("LV", 0, CV), r("NZ", 0, CV), OP.mult)
        lin(r("LM", 0, CV), r("T2", 0, CV), 1.0, float(W), eng="V")
        lin(r("LV", CW, CW + CV), r("LV", 0, CV))

    def later(us, on_v):
        x = t2("T1", 0)
        for j in range(2):
            if on_v:
                tt(x, t2("Q", j), t2("NN", 0), OP.subtract)
                tt(x, x, t2("LV", 0), OP.mult)
                tt(x, x, t2("NN", 0), OP.add)
                p = x
            else:
                p = nb(352, 1)
                mm(p, [(I("If"), t2("Q", j)), (I("Ifn"), t2("NN", 0))])
                tt(x, p, t2("LV", 0), OP.mult)
                p = nb(352, 1)
                mm(p, [(I("If"), x), (I("If"), t2("NN", 0))])
            lin(t2(us, j), p, 0.5, -0.25, eng="V")

    def splice(j):
        a, x = 352 * j, r("T2", CW, 352)
        p = nb(CW, 1)
        mm(p, [(I("If"), r("Q", a + CW, a + 352)), (I("Ifn"), r("Q", a, a + CW))])
        tt(x, p, r("C", 0, CW), OP.mult)
        p = nb(352, 1)
        for b in range(2):
            mm((p[0], CW * b, CW * b + CW, 1), [(I("If"), r("Q", a + CW * b, a + CW * b + CW)), (I("Ifn"), r("P2", CW * b, CW * b + CW)),
                                                (I("Ifn" if b else "If"), x)])
        tt(t2("E", j), p, t2("LV", 0), OP.mult)

    def border(win, land, sb, sem):
        t = r("BT" if sb else "BU", 0, 64)
        for d in range(4):
            o = r("SHU", 4 * d, 4 * d + 4)
            tt(t, r(win, 0, V), r(land, 64 * d, 64 * d + 64), OP.add, off=o)
            scat(r(win, 0, V), o, t)
        if sb:
            lin(r(sb, 0, 256), r(win, 0, V), off=r("SHU", 0, 16))
            send(sb, win, V, sem, False)

    def chain(win, u, first, o, a, b, side):
        if not side:
            for k in range(4):
                if first is None and k == 0:
                    lin(o, r(win, 0, W), off=lst(u, k, a, b))
                else:
                    tt(o, r(win, 0, W), o if k else first, OP.add, off=lst(u, k, a, b))
            return o
        p = nb(b - a)
        mm(p, [(I("I1" if first[0] == "bf" else "If"), first)], stop=False)
        for k in range(4):
            s = slot(b - a)
            lin(s, r(win, 0, W), off=lst(u, k, a, b), eng="S")
            mm(p, [(I("If"), s)], start=False, stop=(k == 3))
        return p

    G = lambda k, a, b: r("GB", W * k + a, W * k + b)
    for a, b in ((0, 512), (512, 1024), (1024, 2048), (2048, W)):
        for k in range(2):
            lin(G(2 + k, a, b), r("XB", 0, W), off=lst("U0", k, a, b))
            tt(G(k, a, b), r("XB", 0, W), G(2 + k, a, b), OP.subtract, off=lst("U0", 2 + k, a, b))
    for j, (a, b) in enumerate(OWN + GHO):
        p = nb(b - a)
        mm(p, [(I("I1"), r("XB", a, b)), const(0, b - a), (I("Inh"), G(2, a, b)), (I("Inh"), G(3, a, b)), (I("Inq"), G(0, a, b)), (I("Inq"), G(1, a, b))])
        rnd(r("D0", a, b), p, M1, j < cfg["rD0"])
        act(r("AB", a, b), r("D0", a, b), AF.Abs)
    for h in range(2):
        a0 = 1280 * h
        for k in range(2):
            relu(r("RL", 1408 * k, 1408 * k + 1280), G(k, a0, a0 + 1280), eng="V")
            for a, b in THIRD:
                p = nb(b - a, 1)
                mm(p, [(I("I1"), G(1 - k, a0 + a, a0 + b)), (I("I1"), G(3 - k, a0 + a, a0 + b)), (I("In1"), G(2 + k, a0 + a, a0 + b))])
                relu(r("RL", 1408 * (2 + k) + a, 1408 * (2 + k) + b), p)
        p = nb(80, 1)
        wrap(p, [(k // 2, "RL", 1408 * k, 16) for k in range(4)])
        ts(r("C", 80 * h, 80 * h + 80), p, 0.0, OP.is_gt)
    for k in range(4):
        ms(r("RL", 1408 * k + 1280, 1408 * k + 1408), 0.0)
    for a, b in HALF:
        lin(r("DS", a, b), r("D0", a, b), 0.25, 191.625)
        lin(r("DS", a, b), r("DS", a, b), 1.0, -192.0)
        ts(r("F0", a, b), r("AB", a, b), col(3), OP.is_ge, 1 / K, OP.max)
    leave("AB", "U0", 0)
    for a, b in HALF:
        tt(r("WN", a, b), r("DS", 0, WZ), r("F0", a, b), OP.mult, off=r("LM", a // 16, b // 16))
    ms(r("WN", V, W), 0.0)
    for j in range(2):
        splice(j)
        lin(t2("HI", j), t2("E", j))
        tt(t2("LO", j), t2("E", j), t2("HI", j), OP.subtract)
        unfold(FN, t2("HI", j), 2 * j)
        unfold(FN, t2("LO", j), 2 * j + 1)
    for a, b in HALF:
        tt(r("H0", a, b), r("D0", 0, WZ), r("F0", a, b), OP.mult, off=r("LM", a // 16, b // 16))
    for j, (a, b) in enumerate(GHO + OWN):
        n = b - a
        gr = [r("GR", 2048 * (j % 2) + 512 * k, 2048 * (j % 2) + 512 * k + n) for k in range(4)]
        for k in range(4):
            lin(gr[k], r("WN", 0, W), off=lst("U0", k, a, b))
        p = nb(n)
        mm(p, ([(I("I16"), r("XB", a, b))] if j else []) + [(I("I256"), x) for x in gr])
        s = slot(n)
        rnd(r("SP", a, b), p, M256, 0 < j <= cfg["rU"], s)
        lin(s, r("SP", a, b), 1 - 1 / K, 3 / 128 if j else 0.0)
        tt(r("X1", a, b) if j else r("HS0", 0, 256), p, s, OP.subtract)
        if not j:
            send("HS0", "LS0", 0, "r1", True)
            lin(r("HP0", 0, 256), r("SP", a, b), -1 / 1024)
    border("X1", "LS0", "E1", "r2")
    send("HP0", "LP0", 0, "r3", True)
    lin(KO, r("LV", 0, CV), BIG, 2 * MID)
    tt(NM, NM, KO, OP.add)
    later("US0", cfg["lat0"])
    for j in (1, 0):
        for a in range(0, 2 * W, 1408):
            lin(r("GB", 2 * W * j + a, 2 * W * j + a + 1408), FN, off=r("POSP" if j else "POSN", a // 16, a // 16 + 88))
        for b in range(2):
            wrap(r("ps%d" % (4 + j), CW * b, CW * b + CW), [(3, "GB", 2 * W + W * b, 16) if j else (2, "GB", b, 32)])
        tt(t2("Q", j), t2("ps%d" % (4 + j), 0), t2("Q", j), OP.add)
        lin(t2("U1", j), t2("Q", j), 0.5, -0.25, eng="V")
    lin(r("QK", 0, 704), r("Q", 0, 704), 1.0, MID)
    lin(t2("G", 0), t2("Q", 0), eng="V")
    pos(t2("POS1", 0), t2("G", 0), 352, 5, CW, "J1", "J2")

    H = lambda k, a, b: r("GH", W * k + a, W * k + b)
    byp = ([(2, j) for j in range(6)] + [(3, j) for j in (1, 3, 5, 0, 2, 4)])[:cfg["ph"]]
    for j, (a, b) in enumerate(OWN + GHO):
        for k in (2, 3, 0, 1):
            if (k, j) in byp:
                s = slot(b - a)
                lin(s, r("X1", 0, W), 16.0, 0.375, off=lst("U1", k, a, b), eng="S")
                cast(H(k, a, b), s)
            else:
                lin(H(k, a, b), r("X1", 0, W), 16.0, 0.375, off=lst("U1", k, a, b), eng="V")
    ms(r("DQ", W, WZ), 0.0)
    for j, (a, b) in enumerate(OWN + GHO):
        p = nb(b - a)
        mm(p, [(I("I4"), r("X1", a, b)), const(1, b - a)] + [(I("Jn16"), H(k, a, b)) for k in (2, 3, 0, 1)])
        rnd(r("DQ", a, b), p, M4, j < cfg["rDQ"])
        act(r("A32", a, b), r("DQ", a, b), AF.Abs, 4.0)
        act(r("PSI", a, b), r("A32", a, b), AF.Relu, -1.0, 255.0)
    for a, b in HALF:
        if cfg["sig"]:
            act(r("CUT", a, b), r("A32", a, b), AF.Sigmoid, -256.0, col(4))
        else:
            ts(r("CUT", a, b), r("A32", a, b), col(3), OP.is_lt)
    nt = 0
    for h in range(2):
        a0, parts, level = 1280 * h, [], 0.0
        for k, (x, y) in enumerate(((0, 2), (1, 3), (1, 2), (0, 3))):
            on_v = 2 * k + h < cfg["cV"]
            parts.append((k // 2 if on_v else 1 - k // 2, "RL", 1408 * k, 16))
            level += 0.0 if on_v else 8192.0 * 4080 * (1 if k // 2 else -1)
            for a, b in THIRD:
                p = nb(b - a, 1)
                mm(p, [(I("J1h"), H(x, a0 + a, a0 + b)), (I("Jn1"), H(y, a0 + a, a0 + b))])
                nt += 1
                t, o = r("TMP", 512 * (nt % 2), 512 * (nt % 2) + b - a), r("RL", 1408 * k + a, 1408 * k + b)
                act(o if on_v else t, p, AF.Abs)
                if not on_v:
                    act(o, t, AF.Relu, -1.0, 255.0)
            if on_v:
                ts(r("RL", 1408 * k, 1408 * k + 1280), r("RL", 1408 * k, 1408 * k + 1280), 255.0, OP.min)
        p = nb(80, 1)
        wrap(p, parts)
        ts(r("C", 80 * h, 80 * h + 80), p, level, OP.is_gt)
    leave("PSI", "U1", 1)
    for a, b in HALF:
        tt(r("DC", a, b), r("DQ", 0, WZ), r("CUT", a, b), OP.mult, off=r("LM", a // 16, b // 16))
        tt(r("H1", a, b), r("DQ", 0, WZ), r("DC", a, b), OP.subtract, off=r("LM", a // 16, b // 16))
        lin(r("IO", a, b), r("DC", a, b), 1 / 16, -3 / 128)
        rnd(r("DC", a, b), r("IO", a, b), M16, False)
    ms(r("DC", V, W), 0.0)
    chain("DC", "U1", None, r("HS1", 0, 256), V, W, False)
    send("HS1", "LS1", 0, "r4", True)

    def cuts(ns):
        a = 512 * ns
        m = a + (V - a) // 64 * 32
        return [(x, y, True) for x, y in OWN[:ns]] + [(a, m, False), (m, V, False)]
    for a, b, side in cuts(cfg["s3"]):
        p = chain("DC", "U1", r("X1", a, b), r("Y1", a, b), a, b, side)
        if side:
            lin(r("Y1", a, b), p)
    border("H1", "LP0", None, None)
    lin(r("E3", 0, 256), r("SP", 0, V), -1 / 1024, off=r("SHU", 0, 16))
    tt(r("E3", 0, 256), r("H1", 0, V), r("E3", 0, 256), OP.add, off=r("SHU", 0, 16))
    border("Y1", "LS1", "E2", "r5")
    p = nb(256)
    mm(p, [(I("I4"), r("E2", 0, 256)), (I("If"), r("E3", 0, 256))])
    lin(r("E3", 0, 256), p)
    send("E3", "Y0", V, "r6", False)
    later("US1", cfg["lat1"])
    splice(0)
    tt(t2("E", 0), t2("E", 0), t2("P2", 0), OP.add)
    unfold(r("FN1", 0, 2 * W), t2("E", 0), 0)
    for a, b, side in cuts(cfg["su"]):
        rnd(r("H1", a, b), chain("Y1", "US1", r("H1", a, b), r("H1", a, b), a, b, side), M4, side and cfg["rH"])
    for a, b in OWN:
        p = nb(512)
        mm(p, [(I("Ink"), r("SP", a, b)), const(2, 512)])
        tt(r("Y0", a, b), p, r("H1", a, b), OP.add)
    for a in (0, 1408):
        for b in range(2):
            lin(r("YN", 2 * a + b, 2 * a + W, 2), r("FN1", 0, 2 * W), off=lst("POS1", b, a, a + 1408))
        y = r("YN", 2 * a, 2 * a + W)
        dma("Y", T.yn[:, 2 * a:2 * a + W], rows(y, 0), [y], [], 90112)
    for j, (a, b) in enumerate(OWN):
        o = r("OUT", a, b)
        rnd(o, chain("Y0", "US0", r("H0", a, b), o, a, b, j < cfg["sf"]), M1, j < cfg["rO"])
        dma("Y", T.yx[:, a:b], ap(o), [o], [], 128 * 512 * 4 * (5 - j))
    return ops


def hazards(ops):
    seen, deps = {}, []
    for i, o in enumerate(ops):
        d = set() if o["after"] is None else {o["after"]}
        acc = [(x[0], 0, 512, w) if x[0][:2] == "ps" else (x[0], x[1], x[2], w) for l, w in ((o["rd"], False), (o["wr"], True)) for x in l]
        for n, a, b, w in acc:
            for j, a2, b2, w2 in seen.get(n, []):
                if a < b2 and a2 < b and o["kind"] != "recv":
                    if w and w2 and None not in (o["tag"], ops[j]["tag"]) and o["tag"] != ops[j]["tag"]:
                        continue
                    if w or w2 or (n[:2] == "ps" and (o["eng"] != ops[j]["eng"] or len(o["eng"]) > 1)):
                        d.add(j)
        for n, a, b, w in acc:
            l = seen.setdefault(n, [])
            if w and o["tag"] is None:
                l[:] = [e for e in l if not (a <= e[1] and e[2] <= b)]
            l.append((i, a, b, w))
        d.discard(i)
        deps.append(sorted(d))
    return deps


def schedule(ops, deps, more, pens):
    n, hop = len(ops), COST["hop"]
    succ = [[] for _ in range(n)]
    for i in range(n):
        for j in deps[i]:
            succ[j].append(i)
    way = [0.0] * n
    for i in range(n - 1, -1, -1):
        way[i] = min(list(ops[i]["cost"].values()) or [0.0]) + ops[i]["lat"] + max([way[j] + hop for j in succ[i]] + [0.0])
    free = {e: 0.0 for e in "VSPGY "}
    done = [0.0] * n
    left = [len(d) for d in deps]
    ready = {i: 0.0 for i in range(n) if not deps[i]}
    order = []
    while ready:
        best = None
        for i, t in ready.items():
            en = ops[i]["eng"] or " "
            for e in en:
                s = max(t, free[e])
                key = (round((s + (pens[i] if e == "V" and len(en) > 1 else 0.0)) / 150.0), -way[i] - more[i], i, e, s)
                if best is None or key < best:
                    best = key
        i, e, s = best[2:]
        del ready[i]
        c = ops[i]["cost"].get(e, 0.0)
        if e != " ":
            free[e] = s + c
        done[i] = s + c + ops[i]["lat"]
        order.append((i, e, s))
        for j in succ[i]:
            left[j] -= 1
            if left[j] == 0:
                ready[j] = max(done[k] for k in deps[j]) + hop
    return order, done


def replay(ops, deps, order, hop):
    free, done = {e: 0.0 for e in "VSPGY "}, [0.0] * len(ops)
    for i, e, _ in order:
        s = max([free[e]] + [done[j] + hop for j in deps[i]])
        c = ops[i]["cost"].get(e, 0.0)
        if e != " ":
            free[e] = s + c
        done[i] = s + c + ops[i]["lat"]
    return max(done)


def search(ops, deps, rounds, vpen, others):
    n = len(ops)
    more, pens = [0.0] * n, [vpen] * n

    def run(m, p):
        s = schedule(ops, deps, m, p)
        return s + (max(s[1]) + sum(replay(o, deps, s[0], h) for o, h in others),)
    best = run(more, pens)
    x = [12345]

    def rand():
        x[0] = (x[0] * 1103515245 + 12345) % 2 ** 31
        return x[0] / 2 ** 31
    for _ in range(rounds):
        m, p = list(more), list(pens)
        a, w, shift, kind = int(rand() * n), 1 + int(rand() * rand() * 40), (rand() - 0.5) * 30000 * rand(), rand()
        for i in range(a, min(n, a + w)):
            if kind < 0.6:
                m[i] += shift
            else:
                p[i] = max(-1000.0, p[i] + shift / 5)
        s = run(m, p)
        if s[2] <= best[2]:
            best, more, pens = s, m, p
    return best


def plan(g, T, topo):
    if not PLAN:
        def length(c, rounds):
            others = []
            for o in OTHER:
                COST.update(o)
                others.append((build(g, T, topo, 0, c), o["hop"]))
            COST.update(MAIN)
            ops = build(g, T, topo, 0, c)
            return search(ops, hazards(ops), rounds, c["vpen"], others)
        cfg = {k: v[0] for k, v in KNOBS.items()}
        best = length(cfg, 60)[2]
        for k in KNOBS:
            for v in KNOBS[k][1:]:
                t = length(dict(cfg, **{k: v}), 60)[2]
                if t < best:
                    best, cfg = t, dict(cfg, **{k: v})
        PLAN["cfg"], PLAN["order"] = cfg, length(cfg, ROUNDS)
    return PLAN["cfg"], PLAN["order"][0]


def rank_program(g, core, T, topo):
    rank = T.rank_of(core)
    if rank is None:
        return
    cfg, order = plan(g, T, topo)
    ops = build(g, T, topo, rank, cfg)
    deps = hazards(ops)
    q = {"V": g.vector, "S": g.scalar, "P": g.tensor, "G": g, "Y": g.sync}
    count = {e: 0 for e in q}
    waited = {e: {} for e in q}
    mark, ends = {}, {}
    per = len(topo.engines(core, T.cores[(rank + 1) % N])) // (N - 1) * (N - 1)
    for i, e, _ in order:
        o = ops[i]
        if o["kind"] == "recv":
            mark[i] = (o["sem"], per)
            ends[o["sem"]] = per
            continue
        need = {}
        for j in deps[i]:
            if mark[j] is not None and not (e == "P" and ops[j]["eng"] == "P"):
                need[mark[j][0]] = max(need.get(mark[j][0], 0), mark[j][1])
        for s in sorted(need):
            if waited[e].get(s, 0) < need[s]:
                q[e].wait_ge(T.sem[s], need[s])
                waited[e][s] = need[s]
        ins = o["fn"](e)
        if o["kind"] == "send":
            mark[i] = None
            ends["ls"] = ends.get("ls", 0) + per
        else:
            count[e] += o["kind"] == "c"
            mark[i] = (o["sem"], 16) if o["kind"] == "dma" else ("c" + e, count[e])
            ins.then_inc(T.sem[mark[i][0]], 16 if o["kind"] == "dma" else 1)
            ends[mark[i][0]] = mark[i][1]
    for s in sorted(ends):
        g.wait_ge(T.sem[s], ends[s])
